import numpy as np
import ml_dtypes


def mxq(x, axis, fmt="e4m3"):
    dtype, down = {"e4m3": (ml_dtypes.float8_e4m3fn, 7), "e5m2": (ml_dtypes.float8_e5m2, 14)}[fmt]
    v = np.moveaxis(np.asarray(x, np.float32).astype(ml_dtypes.bfloat16).astype(np.float64), axis, -1)
    blocks = v.reshape(v.shape[:-1] + (-1, 32))
    amax = np.abs(blocks).max(-1, keepdims=True)
    byte = np.maximum(np.where(amax > 0, np.frexp(amax)[1] - 1 + 127, 0) - down, 1)
    scale = np.exp2(byte - 127.0)
    codes = (blocks / scale).astype(np.float32).astype(dtype).astype(np.float64)
    return np.moveaxis((codes * scale).reshape(v.shape), -1, axis)


WIDE = False


def mx_kscale(k):
    if not WIDE:
        return np.ones(k)
    levels = np.array([10, -10, 5, -5, 0])
    if k % 512:
        return np.exp2(np.random.permutation(np.resize(levels, k // 32))).repeat(32)
    a = np.empty((k // 512, 16))
    for p in range(k // 512):
        a[p, :8] = np.random.permutation(np.resize(levels, 8))
        for g in range(8):
            far = levels[np.abs(levels - a[p, g]) >= 10]
            a[p, g + 8] = far[np.random.randint(len(far))]
    return np.exp2(a.ravel()).repeat(32)


def f64(x):
    return np.asarray(x).astype(np.float64)


def striped(idx):
    return np.tile(idx.reshape(-1, 16).T, (8, 1)).astype(np.uint16)


def unstriped(offs):
    return offs[:16].T.reshape(-1).astype(np.int64)


def pack_weight(w):
    k, n = w.shape
    w = f64(np.asarray(w, np.float32).astype(ml_dtypes.bfloat16)).reshape(k // 32, 32, n)
    amax = np.abs(w).max(1)
    byte = np.clip(np.where(amax > 0, np.frexp(amax)[1] - 1 + 127 - 7, 1), 1, 254)
    scaled = (w * np.exp2(127.0 - byte)[:, None, :]).reshape(k, n).astype(np.float32)
    words = np.ascontiguousarray(scaled.reshape(k // 512, 128, 4, n).transpose(0, 1, 3, 2)).astype(ml_dtypes.float8_e4m3fn).view(np.uint8)
    return words, np.ascontiguousarray(byte.astype(np.uint8).reshape(k // 512, 16, n))


def unpack_weight(words, scales):
    g, p, n, _ = words.shape
    vals = np.ascontiguousarray(words).view(ml_dtypes.float8_e4m3fn).astype(np.float64) * np.repeat(np.exp2(scales.astype(np.float64) - 127.0), 8, axis=1)[..., None]
    return vals.transpose(0, 1, 3, 2).reshape(g * 512, n)


def sigmoid(v):
    return 1.0 / (1.0 + np.exp(-np.maximum(v, -700.0)))

def planes(y):
    n, m = y.shape
    v = y.astype(np.float32).astype(ml_dtypes.bfloat16).astype(np.float64).reshape(n // 32, 32, m)
    top = np.abs(v).max(1)
    byte = np.clip(np.where(top > 0, np.frexp(top)[1] - 1 + 127 - 7, 1), 1, 254)
    codes = (v * np.exp2(127.0 - byte)[:, None, :]).reshape(n, m).astype(np.float32).astype(ml_dtypes.float8_e4m3fn).view(np.uint8)
    words = codes.reshape(n // 512, 128, 4, m).transpose(0, 1, 3, 2)
    return np.ascontiguousarray(words), np.ascontiguousarray(byte.astype(np.uint8).reshape(n // 512, 16, m))


K, T, S, V, N = 512, 1024, 512, 256, 512


def setup_inputs():
    n = np.random.standard_normal
    s = mx_kscale(K)[:, None]
    packed_xT = pack_weight(n((K, T)) * s)
    return {
        "x_words": packed_xT[0],
        "x_scales": packed_xT[1],
        "w1": (n((K, N)) / np.sqrt(K) / s).astype(np.float32),
        "offs": striped(np.random.permutation(T)[:S]),
    }


def reference(x_words, x_scales, w1, offs):
    xq = unpack_weight(x_words, x_scales)[:, unstriped(offs)]
    y = sigmoid(mxq(f64(w1), 0, "e4m3").T @ xq)
    out_0 = y[:, :V] * y[:, V:2 * V]
    return (out_0,) + planes(out_0)

@@ -1,0 +1,152 @@
+from contextlib import ExitStack
+
+import concourse.mybir as mybir
+
+F32 = mybir.dt.float32
+BF16 = mybir.dt.bfloat16
+I32 = mybir.dt.int32
+U32 = mybir.dt.uint32
+U16 = mybir.dt.uint16
+U8 = mybir.dt.uint8
+FP8X4 = mybir.dt.float8_e4m3fn_x4
+SIGMOID = mybir.ActivationFunctionType.Sigmoid
+MULT = mybir.AluOpType.mult
+
+P = 128
+K, T, S, V, N = 512, 1024, 512, 256, 512
+FLOPS = 2 * K * N * S
+HALF = 128
+SCALAR_SHARE = (64, 20)
+
+
+def tile_picked_andpool_none_po_kernel(tc, x_words, x_scales, w1, offs, out_0, out_1, out_2):
+    nc = tc.nc
+    with ExitStack() as ctx:
+        keep = ctx.enter_context(tc.tile_pool(name="keep", bufs=1))
+        reuse = ctx.enter_context(tc.tile_pool(name="reuse", bufs=1))
+        psum = ctx.enter_context(tc.psum_pool(name="psum", bufs=1))
+
+        offsets = keep.tile([P, S // 16], U16, name="offsets")
+        nc.sync.dma_start(offsets[:], offs)
+
+        xs = reuse.tile([P, T], U8, name="xs", align_bytes=64, offset=768)
+        for q in range(4):
+            nc.sync.dma_start(xs[32 * q : 32 * q + 32, :].bitcast(I32), x_scales[0][4 * q : 4 * q + 4, :].bitcast(I32).unsqueeze(0).to_broadcast([8, 4, T // 4]))
+        w_view = w1.rearrange("(p j) n -> p j n", j=4)
+        w_raw = []
+        for c in range(2):
+            raw = reuse.tile([P, 4, 256], F32, name=f"w_raw{c}", align_bytes=64, offset=8192 - 4096 * c)
+            nc.sync.dma_start(raw[:], w_view[:, :, 256 * c : 256 * (c + 1)])
+            w_raw.append(raw)
+        xw = keep.tile([P, T], U32, name="xw", align_bytes=64)
+        nc.sync.dma_start(xw[:].bitcast(I32), x_words[0].rearrange("p n t -> p (n t)").bitcast(I32))
+
+        warm_in = keep.tile([P, 1], F32, name="warm_in")
+        warm_out = keep.tile([P, 1], F32, name="warm_out")
+        nc.vector.memset(warm_in[:], 0.0)
+        nc.scalar.activation(warm_out[:], warm_in[:], SIGMOID)
+
+        gs = keep.tile([P, S], U8, name="gs", align_bytes=64)
+        nc.vector.tensor_copy(gs[:], xs[:].indirect(offsets[:]))
+
+        w_codes = keep.tile([P, 4, P], U32, name="w_codes", align_bytes=64)
+        w_scales = reuse.tile([P, 4, P], U8, name="w_scales", align_bytes=64, offset=1024)
+
+        def quantize_w(c, t, values):
+            nc.vector.quantize_mx(
+                out=w_codes[:, t, 64 * c : 64 * (c + 1)].bitcast(FP8X4),
+                scales=w_scales[:, t, 64 * c : 64 * (c + 1)],
+                in_=values.rearrange("p m j -> p (m j)"),
+            )
+
+        src = [raw[:].rearrange("p j (m t) -> p m j t", t=4) for raw in w_raw]
+        grouped0 = keep.tile([P, 4, 64, 4], BF16, name="grouped0", align_bytes=64)
+        grouped1 = reuse.tile([P, 4, 64, 4], BF16, name="grouped1", align_bytes=64, offset=1536)
+        dst = [g[:].rearrange("p t m j -> p m j t") for g in (grouped0, grouped1)]
+
+        picked = {}
+
+        def pick(h, d):
+            first = V * d + HALF * h
+            picked[h, d] = reuse.tile([P, HALF], U32, name=f"picked{h}{d}", align_bytes=64, offset=4096 + 1024 * h + 512 * d)
+            nc.vector.tensor_copy(picked[h, d][:], xw[:].indirect(offsets[:, first // 16 : (first + HALF) // 16]))
+
+        nc.scalar.copy(dst[0], src[0])
+        nc.vector.tensor_copy(dst[1][:, 22:], src[1][:, 22:])
+        nc.scalar.copy(dst[1][:, :22], src[1][:, :22])
+        for c, g in enumerate((grouped0, grouped1)):
+            for t in range(4):
+                quantize_w(c, t, g[:, t])
+        for h in range(2):
+            for d in range(2):
+                pick(h, d)
+
+        o_codes = keep.tile([P, V], U32, name="o_codes", align_bytes=64)
+        o_scales = keep.tile([P, V], U8, name="o_scales", align_bytes=64)
+        out_view = out_0.rearrange("(p t) v -> p t v", t=4)
+
+        def product(bank, h, d, t):
+            first = V * d + HALF * h
+            nc.tensor.matmul_mx(
+                out=bank,
+                lhsT=w_codes[:, t, :].bitcast(FP8X4),
+                lhsT_scale=w_scales[:, t, :],
+                rhs=picked[h, d][:].bitcast(FP8X4),
+                rhs_scale=gs[:, first : first + HALF],
+                start=True,
+                stop=True,
+            )
+
+        def truth_of(name, pair):
+            bank = psum.tile([P, 2, HALF], F32, name=f"bank{name}")
+            for e, (h, d, t) in enumerate(pair):
+                product(bank[:, e, :], h, d, t)
+            truth = keep.tile([P, 2, HALF], F32, name=f"truth{name}", align_bytes=64)
+            nc.scalar.activation(truth[:], bank[:], SIGMOID)
+            return truth
+
+        def quantize_half(h, rounded):
+            cols = slice(HALF * h, HALF * (h + 1))
+            nc.vector.quantize_mx(
+                out=o_codes[:, cols].bitcast(FP8X4),
+                scales=o_scales[:, cols],
+                in_=rounded[:].rearrange("p v t -> p (v t)"),
+            )
+
+        def round_cols(copy, rounded, prod, lo, hi):
+            copy(
+                rounded[:, lo:hi, :].rearrange("p (c i) t -> p c t i", i=4),
+                prod[:, :, lo:hi].rearrange("p t (c i) -> p c t i", i=4),
+            )
+
+        words_view = out_1[0].rearrange("p n t -> p (n t)").bitcast(I32)
+        y = {}
+        for u in range(2):
+            for d in range(2):
+                y[d, u] = truth_of(f"a{d}{u}", [(0, d, 2 * u), (0, d, 2 * u + 1)])
+        both = [truth_of(f"b{t}", [(1, 0, t), (1, 1, t)]) for t in range(4)]
+        prod = [keep.tile([P, 4, HALF], F32, name=f"prod{h}", align_bytes=64) for h in range(2)]
+        rounded = [keep.tile([P, HALF, 4], BF16, name=f"rounded{h}", align_bytes=64) for h in range(2)]
+
+        def join1(t):
+            nc.vector.tensor_tensor(prod[1][:, t, :], both[t][:, 0, :], both[t][:, 1, :], MULT)
+
+        for u in range(2):
+            nc.vector.tensor_tensor(prod[0][:, 2 * u : 2 * u + 2, :], y[0, u][:], y[1, u][:], MULT)
+        nc.sync.dma_start(out_view[:, :, :HALF], prod[0][:])
+        join1(0)
+        round_cols(nc.vector.tensor_copy, rounded[0], prod[0], 0, HALF)
+        join1(1)
+        nc.sync.dma_start(out_view[:, 0:2, HALF:], prod[1][:, 0:2, :])
+        quantize_half(0, rounded[0])
+        nc.sync.dma_start(words_view[:, :HALF], o_codes[:, :HALF].bitcast(I32))
+        join1(2)
+        join1(3)
+        nc.sync.dma_start(out_view[:, 2:4, HALF:], prod[1][:, 2:4, :])
+        round_cols(nc.vector.tensor_copy, rounded[1], prod[1], 40, HALF)
+        round_cols(nc.scalar.copy, rounded[1], prod[1], 0, 40)
+        quantize_half(1, rounded[1])
+        nc.scalar.dma_start(words_view[:, HALF:], o_codes[:, HALF:].bitcast(I32))
+        for q in range(4):
+            queue = nc.sync if q % 2 == 0 else nc.scalar
+            queue.dma_start(out_2[0][4 * q : 4 * q + 4, :].bitcast(I32), o_scales[32 * q : 32 * q + 4, :].bitcast(I32))

@@ -29,17 +29,16 @@ def tile_picked_andpool_none_po_kernel(tc, x_words, x_scales, w1, offs, out_0, o
         offsets = keep.tile([P, S // 16], U16, name="offsets")
         nc.sync.dma_start(offsets[:], offs)
 
-        xs = reuse.tile([P, T], U8, name="xs", align_bytes=64, offset=768)
-        for q in range(4):
-            nc.sync.dma_start(xs[32 * q : 32 * q + 32, :].bitcast(I32), x_scales[0][4 * q : 4 * q + 4, :].bitcast(I32).unsqueeze(0).to_broadcast([8, 4, T // 4]))
+        xs = keep.tile([P, T], U8, name="xs", align_bytes=64)
+        nc.vector.memset(xs[:].bitcast(I32), 0)
         w_view = w1.rearrange("(p j) n -> p j n", j=4)
-        w_raw = []
-        for c in range(2):
-            raw = reuse.tile([P, 4, 256], F32, name=f"w_raw{c}", align_bytes=64, offset=8192 - 4096 * c)
-            nc.sync.dma_start(raw[:], w_view[:, :, 256 * c : 256 * (c + 1)])
-            w_raw.append(raw)
+        w_raw = reuse.tile([P, 4, N], F32, name="w_raw", align_bytes=64, offset=0)
+        for a in range(2):
+            nc.sync.dma_start(w_raw[:, 2 * a : 2 * a + 2, :], w_view[:, 2 * a : 2 * a + 2, :])
         xw = keep.tile([P, T], U32, name="xw", align_bytes=64)
         nc.sync.dma_start(xw[:].bitcast(I32), x_words[0].rearrange("p n t -> p (n t)").bitcast(I32))
+        for q in range(4):
+            nc.scalar.dma_start(xs[32 * q : 32 * q + 4, :].bitcast(I32), x_scales[0][4 * q : 4 * q + 4, :].bitcast(I32))
 
         warm_in = keep.tile([P, 1], F32, name="warm_in")
         warm_out = keep.tile([P, 1], F32, name="warm_out")
@@ -50,36 +49,38 @@ def tile_picked_andpool_none_po_kernel(tc, x_words, x_scales, w1, offs, out_0, o
         nc.vector.tensor_copy(gs[:], xs[:].indirect(offsets[:]))
 
         w_codes = keep.tile([P, 4, P], U32, name="w_codes", align_bytes=64)
-        w_scales = reuse.tile([P, 4, P], U8, name="w_scales", align_bytes=64, offset=1024)
+        w_scales = keep.tile([P, 4, P], U8, name="w_scales", align_bytes=64)
+        grouped = [keep.tile([P, 4, 64, 4], BF16, name=f"grouped{c}", align_bytes=64) for c in range(2)]
 
-        def quantize_w(c, t, values):
+        def quantize_w(c, t):
             nc.vector.quantize_mx(
                 out=w_codes[:, t, 64 * c : 64 * (c + 1)].bitcast(FP8X4),
                 scales=w_scales[:, t, 64 * c : 64 * (c + 1)],
-                in_=values.rearrange("p m j -> p (m j)"),
+                in_=grouped[c][:, t].rearrange("p m j -> p (m j)"),
             )
-
-        src = [raw[:].rearrange("p j (m t) -> p m j t", t=4) for raw in w_raw]
-        grouped0 = keep.tile([P, 4, 64, 4], BF16, name="grouped0", align_bytes=64)
-        grouped1 = reuse.tile([P, 4, 64, 4], BF16, name="grouped1", align_bytes=64, offset=1536)
-        dst = [g[:].rearrange("p t m j -> p m j t") for g in (grouped0, grouped1)]
 
         picked = {}
 
         def pick(h, d):
             first = V * d + HALF * h
-            picked[h, d] = reuse.tile([P, HALF], U32, name=f"picked{h}{d}", align_bytes=64, offset=4096 + 1024 * h + 512 * d)
+            picked[h, d] = reuse.tile([P, HALF], U32, name=f"picked{h}{d}", align_bytes=64, offset=1024 * h + 512 * d)
             nc.vector.tensor_copy(picked[h, d][:], xw[:].indirect(offsets[:, first // 16 : (first + HALF) // 16]))
 
-        nc.scalar.copy(dst[0], src[0])
-        nc.vector.tensor_copy(dst[1][:, 22:], src[1][:, 22:])
-        nc.scalar.copy(dst[1][:, :22], src[1][:, :22])
-        for c, g in enumerate((grouped0, grouped1)):
-            for t in range(4):
-                quantize_w(c, t, g[:, t])
-        for h in range(2):
+        for a in range(2):
+            nc.scalar.copy(
+                grouped[0][:, :, :, 2 * a : 2 * a + 2].rearrange("p t (m e) j -> p m t e j", e=2),
+                w_raw[:, 2 * a : 2 * a + 2, :256].rearrange("p j (m e t) -> p m t e j", e=2, t=4),
+            )
+        nc.vector.tensor_copy(
+            grouped[1][:].rearrange("p t m j -> p m j t"),
+            w_raw[:, :, 256:].rearrange("p j (m t) -> p m j t", t=4),
+        )
+        for u in range(2):
+            for c in (1, 0):
+                for t in (2 * u, 2 * u + 1):
+                    quantize_w(c, t)
             for d in range(2):
-                pick(h, d)
+                pick(u, d)
 
         o_codes = keep.tile([P, V], U32, name="o_codes", align_bytes=64)
         o_scales = keep.tile([P, V], U8, name="o_scales", align_bytes=64)
@@ -125,7 +126,8 @@ def tile_picked_andpool_none_po_kernel(tc, x_words, x_scales, w1, offs, out_0, o
             for d in range(2):
                 y[d, u] = truth_of(f"a{d}{u}", [(0, d, 2 * u), (0, d, 2 * u + 1)])
         both = [truth_of(f"b{t}", [(1, 0, t), (1, 1, t)]) for t in range(4)]
-        prod = [keep.tile([P, 4, HALF], F32, name=f"prod{h}", align_bytes=64) for h in range(2)]
+        joined = keep.tile([P, 4, V], F32, name="joined", align_bytes=64)
+        prod = [joined[:, :, HALF * h : HALF * (h + 1)] for h in range(2)]
         rounded = [keep.tile([P, HALF, 4], BF16, name=f"rounded{h}", align_bytes=64) for h in range(2)]
 
         def join1(t):
@@ -133,18 +135,17 @@ def tile_picked_andpool_none_po_kernel(tc, x_words, x_scales, w1, offs, out_0, o
 
         for u in range(2):
             nc.vector.tensor_tensor(prod[0][:, 2 * u : 2 * u + 2, :], y[0, u][:], y[1, u][:], MULT)
-        nc.sync.dma_start(out_view[:, :, :HALF], prod[0][:])
         join1(0)
         round_cols(nc.vector.tensor_copy, rounded[0], prod[0], 0, HALF)
         join1(1)
-        nc.sync.dma_start(out_view[:, 0:2, HALF:], prod[1][:, 0:2, :])
+        nc.sync.dma_start(out_view[:, 0:2, :], joined[:, 0:2, :])
         quantize_half(0, rounded[0])
         nc.sync.dma_start(words_view[:, :HALF], o_codes[:, :HALF].bitcast(I32))
         join1(2)
         join1(3)
-        nc.sync.dma_start(out_view[:, 2:4, HALF:], prod[1][:, 2:4, :])
-        round_cols(nc.vector.tensor_copy, rounded[1], prod[1], 40, HALF)
-        round_cols(nc.scalar.copy, rounded[1], prod[1], 0, 40)
+        nc.sync.dma_start(out_view[:, 2:4, :], joined[:, 2:4, :])
+        round_cols(nc.vector.tensor_copy, rounded[1], prod[1], 32, HALF)
+        round_cols(nc.scalar.copy, rounded[1], prod[1], 0, 32)
         quantize_half(1, rounded[1])
         nc.scalar.dma_start(words_view[:, HALF:], o_codes[:, HALF:].bitcast(I32))
         for q in range(4):

@@ -23,7 +23,6 @@ def tile_picked_andpool_none_po_kernel(tc, x_words, x_scales, w1, offs, out_0, o
     nc = tc.nc
     with ExitStack() as ctx:
         keep = ctx.enter_context(tc.tile_pool(name="keep", bufs=1))
-        reuse = ctx.enter_context(tc.tile_pool(name="reuse", bufs=1))
         psum = ctx.enter_context(tc.psum_pool(name="psum", bufs=1))
 
         offsets = keep.tile([P, S // 16], U16, name="offsets")
@@ -32,13 +31,13 @@ def tile_picked_andpool_none_po_kernel(tc, x_words, x_scales, w1, offs, out_0, o
         xs = keep.tile([P, T], U8, name="xs", align_bytes=64)
         nc.vector.memset(xs[:].bitcast(I32), 0)
         w_view = w1.rearrange("(p j) n -> p j n", j=4)
-        w_raw = reuse.tile([P, 4, N], F32, name="w_raw", align_bytes=64, offset=0)
-        for a in range(2):
-            nc.sync.dma_start(w_raw[:, 2 * a : 2 * a + 2, :], w_view[:, 2 * a : 2 * a + 2, :])
+        w_raw = [keep.tile([P, 4, 256], F32, name=f"w_raw{c}", align_bytes=64) for c in range(2)]
+        nc.sync.dma_start(w_raw[0][:], w_view[:, :, :256])
+        for q in range(4):
+            nc.sync.dma_start(xs[32 * q : 32 * q + 4, :].bitcast(I32), x_scales[0][4 * q : 4 * q + 4, :].bitcast(I32))
+        nc.sync.dma_start(w_raw[1][:], w_view[:, :, 256:])
         xw = keep.tile([P, T], U32, name="xw", align_bytes=64)
         nc.sync.dma_start(xw[:].bitcast(I32), x_words[0].rearrange("p n t -> p (n t)").bitcast(I32))
-        for q in range(4):
-            nc.scalar.dma_start(xs[32 * q : 32 * q + 4, :].bitcast(I32), x_scales[0][4 * q : 4 * q + 4, :].bitcast(I32))
 
         warm_in = keep.tile([P, 1], F32, name="warm_in")
         warm_out = keep.tile([P, 1], F32, name="warm_out")
@@ -50,37 +49,29 @@ def tile_picked_andpool_none_po_kernel(tc, x_words, x_scales, w1, offs, out_0, o
 
         w_codes = keep.tile([P, 4, P], U32, name="w_codes", align_bytes=64)
         w_scales = keep.tile([P, 4, P], U8, name="w_scales", align_bytes=64)
-        grouped = [keep.tile([P, 4, 64, 4], BF16, name=f"grouped{c}", align_bytes=64) for c in range(2)]
-
-        def quantize_w(c, t):
-            nc.vector.quantize_mx(
-                out=w_codes[:, t, 64 * c : 64 * (c + 1)].bitcast(FP8X4),
-                scales=w_scales[:, t, 64 * c : 64 * (c + 1)],
-                in_=grouped[c][:, t].rearrange("p m j -> p (m j)"),
-            )
+        grouped = keep.tile([P, 4, P, 4], BF16, name="grouped", align_bytes=64)
 
         picked = {}
 
         def pick(h, d):
             first = V * d + HALF * h
-            picked[h, d] = reuse.tile([P, HALF], U32, name=f"picked{h}{d}", align_bytes=64, offset=1024 * h + 512 * d)
+            picked[h, d] = keep.tile([P, HALF], U32, name=f"picked{h}{d}", align_bytes=64)
             nc.vector.tensor_copy(picked[h, d][:], xw[:].indirect(offsets[:, first // 16 : (first + HALF) // 16]))
 
-        for a in range(2):
-            nc.scalar.copy(
-                grouped[0][:, :, :, 2 * a : 2 * a + 2].rearrange("p t (m e) j -> p m t e j", e=2),
-                w_raw[:, 2 * a : 2 * a + 2, :256].rearrange("p j (m e t) -> p m t e j", e=2, t=4),
-            )
-        nc.vector.tensor_copy(
-            grouped[1][:].rearrange("p t m j -> p m j t"),
-            w_raw[:, :, 256:].rearrange("p j (m t) -> p m j t", t=4),
-        )
+        src = [raw[:].rearrange("p j (m t) -> p m j t", t=4) for raw in w_raw]
+        dst = [grouped[:, :, 64 * c : 64 * (c + 1), :].rearrange("p t m j -> p m j t") for c in range(2)]
+        nc.scalar.copy(dst[0], src[0])
+        nc.vector.tensor_copy(dst[1][:, 22:], src[1][:, 22:])
+        nc.scalar.copy(dst[1][:, :22], src[1][:, :22])
         for u in range(2):
-            for c in (1, 0):
-                for t in (2 * u, 2 * u + 1):
-                    quantize_w(c, t)
+            nc.vector.quantize_mx(
+                out=w_codes[:, 2 * u : 2 * u + 2, :].rearrange("p t m -> p (t m)").bitcast(FP8X4),
+                scales=w_scales[:, 2 * u : 2 * u + 2, :].rearrange("p t m -> p (t m)"),
+                in_=grouped[:, 2 * u : 2 * u + 2].rearrange("p t m j -> p (t m j)"),
+            )
+        for h in range(2):
             for d in range(2):
-                pick(u, d)
+                pick(h, d)
 
         o_codes = keep.tile([P, V], U32, name="o_codes", align_bytes=64)
         o_scales = keep.tile([P, V], U8, name="o_scales", align_bytes=64)
@@ -125,7 +116,13 @@ def tile_picked_andpool_none_po_kernel(tc, x_words, x_scales, w1, offs, out_0, o
         for u in range(2):
             for d in range(2):
                 y[d, u] = truth_of(f"a{d}{u}", [(0, d, 2 * u), (0, d, 2 * u + 1)])
-        both = [truth_of(f"b{t}", [(1, 0, t), (1, 1, t)]) for t in range(4)]
+        both = [truth_of(f"b{t}", [(1, 0, t), (1, 1, t)]) for t in range(3)]
+        last = keep.tile([P, 2, HALF], F32, name="last", align_bytes=64)
+        for d in range(2):
+            bank = psum.tile([P, 2, HALF], F32, name=("banka00", "bankb3")[d])
+            product(bank[:, 0, :], 1, d, 3)
+            nc.scalar.activation(last[:, d, :], bank[:, 0, :], SIGMOID)
+        both.append(last)
         joined = keep.tile([P, 4, V], F32, name="joined", align_bytes=64)
         prod = [joined[:, :, HALF * h : HALF * (h + 1)] for h in range(2)]
         rounded = [keep.tile([P, HALF, 4], BF16, name=f"rounded{h}", align_bytes=64) for h in range(2)]

@@ -16,7 +16,7 @@ P = 128
 K, T, S, V, N = 512, 1024, 512, 256, 512
 FLOPS = 2 * K * N * S
 HALF = 128
-SCALAR_SHARE = (64, 20)
+PIECES = ((0, 48, 48), (48, 96, 36), (96, 128, 10))
 
 
 def tile_picked_andpool_none_po_kernel(tc, x_words, x_scales, w1, offs, out_0, out_1, out_2):
@@ -31,18 +31,14 @@ def tile_picked_andpool_none_po_kernel(tc, x_words, x_scales, w1, offs, out_0, o
         xs = keep.tile([P, T], U8, name="xs", align_bytes=64)
         nc.vector.memset(xs[:].bitcast(I32), 0)
         w_view = w1.rearrange("(p j) n -> p j n", j=4)
-        w_raw = [keep.tile([P, 4, 256], F32, name=f"w_raw{c}", align_bytes=64) for c in range(2)]
-        nc.sync.dma_start(w_raw[0][:], w_view[:, :, :256])
+        w_raw = [keep.tile([P, 4, 4 * (hi - lo)], F32, name=f"w_raw{lo}", align_bytes=64) for lo, hi, share in PIECES]
+        nc.sync.dma_start(w_raw[0][:], w_view[:, :, : 4 * PIECES[0][1]])
         for q in range(4):
             nc.sync.dma_start(xs[32 * q : 32 * q + 4, :].bitcast(I32), x_scales[0][4 * q : 4 * q + 4, :].bitcast(I32))
-        nc.sync.dma_start(w_raw[1][:], w_view[:, :, 256:])
+        for raw, (lo, hi, share) in zip(w_raw[1:], PIECES[1:]):
+            nc.sync.dma_start(raw[:], w_view[:, :, 4 * lo : 4 * hi])
         xw = keep.tile([P, T], U32, name="xw", align_bytes=64)
         nc.sync.dma_start(xw[:].bitcast(I32), x_words[0].rearrange("p n t -> p (n t)").bitcast(I32))
-
-        warm_in = keep.tile([P, 1], F32, name="warm_in")
-        warm_out = keep.tile([P, 1], F32, name="warm_out")
-        nc.vector.memset(warm_in[:], 0.0)
-        nc.scalar.activation(warm_out[:], warm_in[:], SIGMOID)
 
         gs = keep.tile([P, S], U8, name="gs", align_bytes=64)
         nc.vector.tensor_copy(gs[:], xs[:].indirect(offsets[:]))
@@ -58,11 +54,12 @@ def tile_picked_andpool_none_po_kernel(tc, x_words, x_scales, w1, offs, out_0, o
             picked[h, d] = keep.tile([P, HALF], U32, name=f"picked{h}{d}", align_bytes=64)
             nc.vector.tensor_copy(picked[h, d][:], xw[:].indirect(offsets[:, first // 16 : (first + HALF) // 16]))
 
-        src = [raw[:].rearrange("p j (m t) -> p m j t", t=4) for raw in w_raw]
-        dst = [grouped[:, :, 64 * c : 64 * (c + 1), :].rearrange("p t m j -> p m j t") for c in range(2)]
-        nc.scalar.copy(dst[0], src[0])
-        nc.vector.tensor_copy(dst[1][:, 22:], src[1][:, 22:])
-        nc.scalar.copy(dst[1][:, :22], src[1][:, :22])
+        for raw, (lo, hi, share) in zip(w_raw, PIECES):
+            src = raw[:].rearrange("p j (m t) -> p m j t", t=4)
+            dst = grouped[:, :, lo:hi, :].rearrange("p t m j -> p m j t")
+            nc.scalar.copy(dst[:, :share], src[:, :share])
+            if share < hi - lo:
+                nc.vector.tensor_copy(dst[:, share:], src[:, share:])
         for u in range(2):
             nc.vector.quantize_mx(
                 out=w_codes[:, 2 * u : 2 * u + 2, :].rearrange("p t m -> p (t m)").bitcast(FP8X4),

@@ -16,6 +16,7 @@ P = 128
 K, T, S, V, N = 512, 1024, 512, 256, 512
 FLOPS = 2 * K * N * S
 HALF = 128
+QUARTER = 64
 PIECES = ((0, 48, 48), (48, 96, 36), (96, 128, 10))
 
 
@@ -28,13 +29,20 @@ def tile_picked_andpool_none_po_kernel(tc, x_words, x_scales, w1, offs, out_0, o
         offsets = keep.tile([P, S // 16], U16, name="offsets")
         nc.sync.dma_start(offsets[:], offs)
 
-        xs = keep.tile([P, T], U8, name="xs", align_bytes=64)
-        nc.vector.memset(xs[:].bitcast(I32), 0)
         w_view = w1.rearrange("(p j) n -> p j n", j=4)
         w_raw = [keep.tile([P, 4, 4 * (hi - lo)], F32, name=f"w_raw{lo}", align_bytes=64) for lo, hi, share in PIECES]
         nc.sync.dma_start(w_raw[0][:], w_view[:, :, : 4 * PIECES[0][1]])
+
+        xs = keep.tile([P, T], U8, name="xs", align_bytes=64)
+        nc.vector.memset(xs[:].bitcast(I32), 0)
+        warm_in = keep.tile([P, 1], F32, name="warm_in")
+        warm_out = keep.tile([P, 1], F32, name="warm_out")
+        nc.vector.memset(warm_in[:], 0.0)
+
         for q in range(4):
-            nc.sync.dma_start(xs[32 * q : 32 * q + 4, :].bitcast(I32), x_scales[0][4 * q : 4 * q + 4, :].bitcast(I32))
+            queue = nc.sync if q < 2 else nc.scalar
+            queue.dma_start(xs[32 * q : 32 * q + 4, :].bitcast(I32), x_scales[0][4 * q : 4 * q + 4, :].bitcast(I32))
+        nc.scalar.activation(warm_out[:], warm_in[:], SIGMOID)
         for raw, (lo, hi, share) in zip(w_raw[1:], PIECES[1:]):
             nc.sync.dma_start(raw[:], w_view[:, :, 4 * lo : 4 * hi])
         xw = keep.tile([P, T], U32, name="xw", align_bytes=64)
@@ -46,13 +54,7 @@ def tile_picked_andpool_none_po_kernel(tc, x_words, x_scales, w1, offs, out_0, o
         w_codes = keep.tile([P, 4, P], U32, name="w_codes", align_bytes=64)
         w_scales = keep.tile([P, 4, P], U8, name="w_scales", align_bytes=64)
         grouped = keep.tile([P, 4, P, 4], BF16, name="grouped", align_bytes=64)
-
-        picked = {}
-
-        def pick(h, d):
-            first = V * d + HALF * h
-            picked[h, d] = keep.tile([P, HALF], U32, name=f"picked{h}{d}", align_bytes=64)
-            nc.vector.tensor_copy(picked[h, d][:], xw[:].indirect(offsets[:, first // 16 : (first + HALF) // 16]))
+        paired_scales = keep.tile([P, 2, 2, QUARTER], U8, name="paired_scales", align_bytes=64)
 
         for raw, (lo, hi, share) in zip(w_raw, PIECES):
             src = raw[:].rearrange("p j (m t) -> p m j t", t=4)
@@ -60,88 +62,110 @@ def tile_picked_andpool_none_po_kernel(tc, x_words, x_scales, w1, offs, out_0, o
             nc.scalar.copy(dst[:, :share], src[:, :share])
             if share < hi - lo:
                 nc.vector.tensor_copy(dst[:, share:], src[:, share:])
+        for q in range(2):
+            nc.sync.dma_start(
+                paired_scales[:, q].bitcast(I32),
+                gs[:].bitcast(I32).rearrange("p (d q c) -> p q d c", d=2, q=4)[:, 2 + q],
+            )
         for u in range(2):
             nc.vector.quantize_mx(
                 out=w_codes[:, 2 * u : 2 * u + 2, :].rearrange("p t m -> p (t m)").bitcast(FP8X4),
                 scales=w_scales[:, 2 * u : 2 * u + 2, :].rearrange("p t m -> p (t m)"),
                 in_=grouped[:, 2 * u : 2 * u + 2].rearrange("p t m j -> p (t m j)"),
             )
-        for h in range(2):
-            for d in range(2):
-                pick(h, d)
+
+        def pick(dst, h, d):
+            first = V * d + HALF * h
+            nc.vector.tensor_copy(dst, xw[:].indirect(offsets[:, first // 16 : (first + HALF) // 16]))
+
+        plain = [keep.tile([P, HALF], U32, name=f"plain{d}", align_bytes=64) for d in range(2)]
+        paired = keep.tile([P, 2, 2, QUARTER], U32, name="paired", align_bytes=64)
+        for d in range(2):
+            pick(plain[d][:], 0, d)
+        for d in range(2):
+            pick(paired[:, :, d, :], 1, d)
 
         o_codes = keep.tile([P, V], U32, name="o_codes", align_bytes=64)
         o_scales = keep.tile([P, V], U8, name="o_scales", align_bytes=64)
         out_view = out_0.rearrange("(p t) v -> p t v", t=4)
+        words_view = out_1[0].rearrange("p n t -> p (n t)").bitcast(I32)
+        left = keep.tile([P, 4, 2, HALF], F32, name="left", align_bytes=64)
+        truth = [keep.tile([P, 4, 2, QUARTER], F32, name=f"truth{q}", align_bytes=64) for q in range(2)]
+        joined = keep.tile([P, 4, V], F32, name="joined", align_bytes=64)
+        rounded = [keep.tile([P, HALF, 4], BF16, name=f"rounded{h}", align_bytes=64) for h in range(2)]
 
-        def product(bank, h, d, t):
-            first = V * d + HALF * h
+        def product(dst, t, codes, scales):
             nc.tensor.matmul_mx(
-                out=bank,
+                out=dst,
                 lhsT=w_codes[:, t, :].bitcast(FP8X4),
                 lhsT_scale=w_scales[:, t, :],
-                rhs=picked[h, d][:].bitcast(FP8X4),
-                rhs_scale=gs[:, first : first + HALF],
+                rhs=codes.bitcast(FP8X4),
+                rhs_scale=scales,
                 start=True,
                 stop=True,
             )
 
-        def truth_of(name, pair):
-            bank = psum.tile([P, 2, HALF], F32, name=f"bank{name}")
-            for e, (h, d, t) in enumerate(pair):
-                product(bank[:, e, :], h, d, t)
-            truth = keep.tile([P, 2, HALF], F32, name=f"truth{name}", align_bytes=64)
-            nc.scalar.activation(truth[:], bank[:], SIGMOID)
-            return truth
+        def left_sigmoids(name, pairs, dst):
+            bank = psum.tile([P, 2, HALF], F32, name=name)
+            for e, (t, d) in enumerate(pairs):
+                product(bank[:, e, :], t, plain[d][:], gs[:, V * d : V * d + HALF])
+            nc.scalar.activation(dst, bank[:], SIGMOID)
 
-        def quantize_half(h, rounded):
+        def right_sigmoids(name, q, lo, hi):
+            bank = psum.tile([P, 2, HALF], F32, name=name)
+            for t in range(lo, hi):
+                product(bank[:, t - lo, :], t, paired[:, q].rearrange("p d c -> p (d c)"), paired_scales[:, q].rearrange("p d c -> p (d c)"))
+            nc.scalar.activation(truth[q][:, lo:hi].rearrange("p t d c -> p t (d c)"), bank[:, : hi - lo, :], SIGMOID)
+
+        def join_left(lo, hi):
+            nc.vector.tensor_tensor(joined[:, lo:hi, :HALF], left[:, lo:hi, 0, :], left[:, lo:hi, 1, :], MULT)
+
+        def columns(q):
+            return slice(HALF + QUARTER * q, HALF + QUARTER * (q + 1))
+
+        def join_right(q, lo, hi):
+            nc.vector.tensor_tensor(joined[:, lo:hi, columns(q)], truth[q][:, lo:hi, 0, :], truth[q][:, lo:hi, 1, :], MULT)
+
+        def interleaved(tile):
+            return tile.rearrange("p (c i) t -> p c t i", i=4)
+
+        def by_fours(rows):
+            return rows.rearrange("p t (c i) -> p c t i", i=4)
+
+        def quantize_half(h):
             cols = slice(HALF * h, HALF * (h + 1))
             nc.vector.quantize_mx(
                 out=o_codes[:, cols].bitcast(FP8X4),
                 scales=o_scales[:, cols],
-                in_=rounded[:].rearrange("p v t -> p (v t)"),
+                in_=rounded[h][:].rearrange("p v t -> p (v t)"),
             )
 
-        def round_cols(copy, rounded, prod, lo, hi):
-            copy(
-                rounded[:, lo:hi, :].rearrange("p (c i) t -> p c t i", i=4),
-                prod[:, :, lo:hi].rearrange("p t (c i) -> p c t i", i=4),
-            )
+        left_sigmoids("bank0", [(0, 0), (1, 0)], left[:, 0:2, 0, :])
+        left_sigmoids("bank1", [(0, 1), (1, 1)], left[:, 0:2, 1, :])
+        left_sigmoids("bank2", [(2, 0), (2, 1)], left[:, 2, :, :])
+        left_sigmoids("bank3", [(3, 0), (3, 1)], left[:, 3, :, :])
+        right_sigmoids("bank4", 0, 0, 2)
+        right_sigmoids("bank5", 0, 2, 4)
+        right_sigmoids("bank6", 1, 0, 2)
+        right_sigmoids("bank0", 1, 2, 3)
+        right_sigmoids("bank7", 1, 3, 4)
 
-        words_view = out_1[0].rearrange("p n t -> p (n t)").bitcast(I32)
-        y = {}
-        for u in range(2):
-            for d in range(2):
-                y[d, u] = truth_of(f"a{d}{u}", [(0, d, 2 * u), (0, d, 2 * u + 1)])
-        both = [truth_of(f"b{t}", [(1, 0, t), (1, 1, t)]) for t in range(3)]
-        last = keep.tile([P, 2, HALF], F32, name="last", align_bytes=64)
-        for d in range(2):
-            bank = psum.tile([P, 2, HALF], F32, name=("banka00", "bankb3")[d])
-            product(bank[:, 0, :], 1, d, 3)
-            nc.scalar.activation(last[:, d, :], bank[:, 0, :], SIGMOID)
-        both.append(last)
-        joined = keep.tile([P, 4, V], F32, name="joined", align_bytes=64)
-        prod = [joined[:, :, HALF * h : HALF * (h + 1)] for h in range(2)]
-        rounded = [keep.tile([P, HALF, 4], BF16, name=f"rounded{h}", align_bytes=64) for h in range(2)]
-
-        def join1(t):
-            nc.vector.tensor_tensor(prod[1][:, t, :], both[t][:, 0, :], both[t][:, 1, :], MULT)
-
-        for u in range(2):
-            nc.vector.tensor_tensor(prod[0][:, 2 * u : 2 * u + 2, :], y[0, u][:], y[1, u][:], MULT)
-        join1(0)
-        round_cols(nc.vector.tensor_copy, rounded[0], prod[0], 0, HALF)
-        join1(1)
-        nc.sync.dma_start(out_view[:, 0:2, :], joined[:, 0:2, :])
-        quantize_half(0, rounded[0])
-        nc.sync.dma_start(words_view[:, :HALF], o_codes[:, :HALF].bitcast(I32))
-        join1(2)
-        join1(3)
-        nc.sync.dma_start(out_view[:, 2:4, :], joined[:, 2:4, :])
-        round_cols(nc.vector.tensor_copy, rounded[1], prod[1], 32, HALF)
-        round_cols(nc.scalar.copy, rounded[1], prod[1], 0, 32)
-        quantize_half(1, rounded[1])
-        nc.scalar.dma_start(words_view[:, HALF:], o_codes[:, HALF:].bitcast(I32))
+        join_left(0, 2)
+        join_left(2, 3)
+        join_left(3, 4)
+        nc.sync.dma_start(out_view[:, :, :HALF], joined[:, :, :HALF])
+        join_right(0, 0, 2)
+        nc.vector.tensor_copy(interleaved(rounded[0][:]), by_fours(joined[:, :, :HALF]))
+        join_right(0, 2, 4)
+        quantize_half(0)
+        join_right(1, 0, 2)
+        nc.sync.dma_start(out_view[:, 0:2, HALF:], joined[:, 0:2, HALF:])
+        nc.scalar.copy(interleaved(rounded[1][:, :QUARTER, :]), by_fours(joined[:, :, columns(0)]))
+        nc.vector.tensor_tensor(interleaved(rounded[1][:, QUARTER:, :]), by_fours(truth[1][:, :, 0, :]), by_fours(truth[1][:, :, 1, :]), MULT)
+        join_right(1, 2, 4)
+        nc.scalar.dma_start(out_view[:, 2:4, HALF:], joined[:, 2:4, HALF:])
+        quantize_half(1)
+        nc.sync.dma_start(words_view, o_codes[:].bitcast(I32))
         for q in range(4):
             queue = nc.sync if q % 2 == 0 else nc.scalar
             queue.dma_start(out_2[0][4 * q : 4 * q + 4, :].bitcast(I32), o_scales[32 * q : 32 * q + 4, :].bitcast(I32))

@@ -35,14 +35,9 @@ def tile_picked_andpool_none_po_kernel(tc, x_words, x_scales, w1, offs, out_0, o
 
         xs = keep.tile([P, T], U8, name="xs", align_bytes=64)
         nc.vector.memset(xs[:].bitcast(I32), 0)
-        warm_in = keep.tile([P, 1], F32, name="warm_in")
-        warm_out = keep.tile([P, 1], F32, name="warm_out")
-        nc.vector.memset(warm_in[:], 0.0)
 
         for q in range(4):
-            queue = nc.sync if q < 2 else nc.scalar
-            queue.dma_start(xs[32 * q : 32 * q + 4, :].bitcast(I32), x_scales[0][4 * q : 4 * q + 4, :].bitcast(I32))
-        nc.scalar.activation(warm_out[:], warm_in[:], SIGMOID)
+            nc.sync.dma_start(xs[32 * q : 32 * q + 4, :].bitcast(I32), x_scales[0][4 * q : 4 * q + 4, :].bitcast(I32))
         for raw, (lo, hi, share) in zip(w_raw[1:], PIECES[1:]):
             nc.sync.dma_start(raw[:], w_view[:, :, 4 * lo : 4 * hi])
         xw = keep.tile([P, T], U32, name="xw", align_bytes=64)
@@ -163,9 +158,9 @@ def tile_picked_andpool_none_po_kernel(tc, x_words, x_scales, w1, offs, out_0, o
         nc.scalar.copy(interleaved(rounded[1][:, :QUARTER, :]), by_fours(joined[:, :, columns(0)]))
         nc.vector.tensor_tensor(interleaved(rounded[1][:, QUARTER:, :]), by_fours(truth[1][:, :, 0, :]), by_fours(truth[1][:, :, 1, :]), MULT)
         join_right(1, 2, 4)
-        nc.scalar.dma_start(out_view[:, 2:4, HALF:], joined[:, 2:4, HALF:])
+        nc.sync.dma_start(out_view[:, 2:4, HALF:], joined[:, 2:4, HALF:])
         quantize_half(1)
-        nc.sync.dma_start(words_view, o_codes[:].bitcast(I32))
+        nc.scalar.dma_start(words_view, o_codes[:].bitcast(I32))
         for q in range(4):
             queue = nc.sync if q % 2 == 0 else nc.scalar
             queue.dma_start(out_2[0][4 * q : 4 * q + 4, :].bitcast(I32), o_scales[32 * q : 32 * q + 4, :].bitcast(I32))

@@ -36,8 +36,9 @@ def tile_picked_andpool_none_po_kernel(tc, x_words, x_scales, w1, offs, out_0, o
         xs = keep.tile([P, T], U8, name="xs", align_bytes=64)
         nc.vector.memset(xs[:].bitcast(I32), 0)
 
-        for q in range(4):
-            nc.sync.dma_start(xs[32 * q : 32 * q + 4, :].bitcast(I32), x_scales[0][4 * q : 4 * q + 4, :].bitcast(I32))
+        scale_rows = x_scales[0].rearrange("(q r) c -> r q c", r=4)
+        for r in range(4):
+            nc.sync.dma_start(xs[r:P:32, :].bitcast(I32), scale_rows[r].bitcast(I32))
         for raw, (lo, hi, share) in zip(w_raw[1:], PIECES[1:]):
             nc.sync.dma_start(raw[:], w_view[:, :, 4 * lo : 4 * hi])
         xw = keep.tile([P, T], U32, name="xw", align_bytes=64)

@@ -17,7 +17,7 @@ K, T, S, V, N = 512, 1024, 512, 256, 512
 FLOPS = 2 * K * N * S
 HALF = 128
 QUARTER = 64
-PIECES = ((0, 48, 48), (48, 96, 36), (96, 128, 10))
+PIECES = ((0, 48), (48, 96), (96, 128))
 
 
 def tile_picked_andpool_none_po_kernel(tc, x_words, x_scales, w1, offs, out_0, out_1, out_2):
@@ -30,7 +30,7 @@ def tile_picked_andpool_none_po_kernel(tc, x_words, x_scales, w1, offs, out_0, o
         nc.sync.dma_start(offsets[:], offs)
 
         w_view = w1.rearrange("(p j) n -> p j n", j=4)
-        w_raw = [keep.tile([P, 4, 4 * (hi - lo)], F32, name=f"w_raw{lo}", align_bytes=64) for lo, hi, share in PIECES]
+        w_raw = [keep.tile([P, 4, 4 * (hi - lo)], F32, name=f"w_raw{lo}", align_bytes=64) for lo, hi in PIECES]
         nc.sync.dma_start(w_raw[0][:], w_view[:, :, : 4 * PIECES[0][1]])
 
         xs = keep.tile([P, T], U8, name="xs", align_bytes=64)
@@ -39,7 +39,7 @@ def tile_picked_andpool_none_po_kernel(tc, x_words, x_scales, w1, offs, out_0, o
         scale_rows = x_scales[0].rearrange("(q r) c -> r q c", r=4)
         for r in range(4):
             nc.sync.dma_start(xs[r:P:32, :].bitcast(I32), scale_rows[r].bitcast(I32))
-        for raw, (lo, hi, share) in zip(w_raw[1:], PIECES[1:]):
+        for raw, (lo, hi) in zip(w_raw[1:], PIECES[1:]):
             nc.sync.dma_start(raw[:], w_view[:, :, 4 * lo : 4 * hi])
         xw = keep.tile([P, T], U32, name="xw", align_bytes=64)
         nc.sync.dma_start(xw[:].bitcast(I32), x_words[0].rearrange("p n t -> p (n t)").bitcast(I32))
@@ -52,12 +52,12 @@ def tile_picked_andpool_none_po_kernel(tc, x_words, x_scales, w1, offs, out_0, o
         grouped = keep.tile([P, 4, P, 4], BF16, name="grouped", align_bytes=64)
         paired_scales = keep.tile([P, 2, 2, QUARTER], U8, name="paired_scales", align_bytes=64)
 
-        for raw, (lo, hi, share) in zip(w_raw, PIECES):
-            src = raw[:].rearrange("p j (m t) -> p m j t", t=4)
-            dst = grouped[:, :, lo:hi, :].rearrange("p t m j -> p m j t")
-            nc.scalar.copy(dst[:, :share], src[:, :share])
-            if share < hi - lo:
-                nc.vector.tensor_copy(dst[:, share:], src[:, share:])
+        src = [raw[:].rearrange("p j (m t) -> p m j t", t=4) for raw in w_raw]
+        dst = [grouped[:, :, lo:hi, :].rearrange("p t m j -> p m j t") for lo, hi in PIECES]
+        nc.scalar.copy(dst[0], src[0])
+        for u in range(2):
+            nc.scalar.copy(dst[1][:, :, :, 2 * u : 2 * u + 2], src[1][:, :, :, 2 * u : 2 * u + 2])
+            nc.vector.tensor_copy(dst[2][:, :, :, 2 * u : 2 * u + 2], src[2][:, :, :, 2 * u : 2 * u + 2])
         for q in range(2):
             nc.sync.dma_start(
                 paired_scales[:, q].bitcast(I32),

@@ -162,6 +162,7 @@ def tile_picked_andpool_none_po_kernel(tc, x_words, x_scales, w1, offs, out_0, o
         nc.sync.dma_start(out_view[:, 2:4, HALF:], joined[:, 2:4, HALF:])
         quantize_half(1)
         nc.scalar.dma_start(words_view, o_codes[:].bitcast(I32))
-        for q in range(4):
-            queue = nc.sync if q % 2 == 0 else nc.scalar
-            queue.dma_start(out_2[0][4 * q : 4 * q + 4, :].bitcast(I32), o_scales[32 * q : 32 * q + 4, :].bitcast(I32))
+        out_rows = out_2[0].rearrange("(q r) c -> r q c", r=4)
+        for r in range(4):
+            queue = nc.sync if r % 2 == 0 else nc.scalar
+            queue.dma_start(out_rows[r].bitcast(I32), o_scales[r:P:32, :].bitcast(I32))

@@ -17,7 +17,7 @@ K, T, S, V, N = 512, 1024, 512, 256, 512
 FLOPS = 2 * K * N * S
 HALF = 128
 QUARTER = 64
-PIECES = ((0, 48), (48, 96), (96, 128))
+SHARE = 24
 
 
 def tile_picked_andpool_none_po_kernel(tc, x_words, x_scales, w1, offs, out_0, out_1, out_2):
@@ -30,8 +30,8 @@ def tile_picked_andpool_none_po_kernel(tc, x_words, x_scales, w1, offs, out_0, o
         nc.sync.dma_start(offsets[:], offs)
 
         w_view = w1.rearrange("(p j) n -> p j n", j=4)
-        w_raw = [keep.tile([P, 4, 4 * (hi - lo)], F32, name=f"w_raw{lo}", align_bytes=64) for lo, hi in PIECES]
-        nc.sync.dma_start(w_raw[0][:], w_view[:, :, : 4 * PIECES[0][1]])
+        w_raw = [keep.tile([P, 4, N // 2], F32, name=f"w_raw{h}", align_bytes=64) for h in range(2)]
+        nc.sync.dma_start(w_raw[0][:, 0:3, :], w_view[:, 0:3, : N // 2])
 
         xs = keep.tile([P, T], U8, name="xs", align_bytes=64)
         nc.vector.memset(xs[:].bitcast(I32), 0)
@@ -39,8 +39,8 @@ def tile_picked_andpool_none_po_kernel(tc, x_words, x_scales, w1, offs, out_0, o
         scale_rows = x_scales[0].rearrange("(q r) c -> r q c", r=4)
         for r in range(4):
             nc.sync.dma_start(xs[r:P:32, :].bitcast(I32), scale_rows[r].bitcast(I32))
-        for raw, (lo, hi) in zip(w_raw[1:], PIECES[1:]):
-            nc.sync.dma_start(raw[:], w_view[:, :, 4 * lo : 4 * hi])
+        nc.sync.dma_start(w_raw[0][:, 3, :], w_view[:, 3, : N // 2])
+        nc.sync.dma_start(w_raw[1][:], w_view[:, :, N // 2 :])
         xw = keep.tile([P, T], U32, name="xw", align_bytes=64)
         nc.sync.dma_start(xw[:].bitcast(I32), x_words[0].rearrange("p n t -> p (n t)").bitcast(I32))
 
@@ -52,12 +52,18 @@ def tile_picked_andpool_none_po_kernel(tc, x_words, x_scales, w1, offs, out_0, o
         grouped = keep.tile([P, 4, P, 4], BF16, name="grouped", align_bytes=64)
         paired_scales = keep.tile([P, 2, 2, QUARTER], U8, name="paired_scales", align_bytes=64)
 
-        src = [raw[:].rearrange("p j (m t) -> p m j t", t=4) for raw in w_raw]
-        dst = [grouped[:, :, lo:hi, :].rearrange("p t m j -> p m j t") for lo, hi in PIECES]
-        nc.scalar.copy(dst[0], src[0])
-        for u in range(2):
-            nc.scalar.copy(dst[1][:, :, :, 2 * u : 2 * u + 2], src[1][:, :, :, 2 * u : 2 * u + 2])
-            nc.vector.tensor_copy(dst[2][:, :, :, 2 * u : 2 * u + 2], src[2][:, :, :, 2 * u : 2 * u + 2])
+        def views(lo, hi, t0, t1):
+            h = lo // 64
+            src = w_raw[h][:].rearrange("p j (m t) -> p m j t", t=4)[:, lo - 64 * h : hi - 64 * h, :, t0:t1]
+            dst = grouped[:, t0:t1, lo:hi, :].rearrange("p t m j -> p m j t")
+            return dst, src
+
+        warm_out = keep.tile([P, 1], F32, name="warm_out")
+        nc.scalar.activation(warm_out[:], w_raw[0][:, 0, 0:1], SIGMOID)
+        nc.scalar.copy(*views(0, 64, 0, 4))
+        nc.scalar.copy(*views(64, 64 + SHARE, 0, 2))
+        nc.vector.tensor_copy(*views(64 + SHARE, 128, 0, 2))
+        nc.vector.tensor_copy(*views(64, 128, 2, 4))
         for q in range(2):
             nc.sync.dma_start(
                 paired_scales[:, q].bitcast(I32),
@@ -88,7 +94,7 @@ def tile_picked_andpool_none_po_kernel(tc, x_words, x_scales, w1, offs, out_0, o
         left = keep.tile([P, 4, 2, HALF], F32, name="left", align_bytes=64)
         truth = [keep.tile([P, 4, 2, QUARTER], F32, name=f"truth{q}", align_bytes=64) for q in range(2)]
         joined = keep.tile([P, 4, V], F32, name="joined", align_bytes=64)
-        rounded = [keep.tile([P, HALF, 4], BF16, name=f"rounded{h}", align_bytes=64) for h in range(2)]
+        rounded = keep.tile([P, V, 4], BF16, name="rounded", align_bytes=64)
 
         def product(dst, t, codes, scales):
             nc.tensor.matmul_mx(
@@ -128,12 +134,11 @@ def tile_picked_andpool_none_po_kernel(tc, x_words, x_scales, w1, offs, out_0, o
         def by_fours(rows):
             return rows.rearrange("p t (c i) -> p c t i", i=4)
 
-        def quantize_half(h):
-            cols = slice(HALF * h, HALF * (h + 1))
+        def quantize(lo, hi):
             nc.vector.quantize_mx(
-                out=o_codes[:, cols].bitcast(FP8X4),
-                scales=o_scales[:, cols],
-                in_=rounded[h][:].rearrange("p v t -> p (v t)"),
+                out=o_codes[:, lo:hi].bitcast(FP8X4),
+                scales=o_scales[:, lo:hi],
+                in_=rounded[:, lo:hi, :].rearrange("p v t -> p (v t)"),
             )
 
         left_sigmoids("bank0", [(0, 0), (1, 0)], left[:, 0:2, 0, :])
@@ -151,16 +156,18 @@ def tile_picked_andpool_none_po_kernel(tc, x_words, x_scales, w1, offs, out_0, o
         join_left(3, 4)
         nc.sync.dma_start(out_view[:, :, :HALF], joined[:, :, :HALF])
         join_right(0, 0, 2)
-        nc.vector.tensor_copy(interleaved(rounded[0][:]), by_fours(joined[:, :, :HALF]))
+        nc.vector.tensor_copy(interleaved(rounded[:, :QUARTER, :]), by_fours(joined[:, :, :QUARTER]))
         join_right(0, 2, 4)
-        quantize_half(0)
+        nc.vector.tensor_copy(interleaved(rounded[:, QUARTER:HALF, :]), by_fours(joined[:, :, QUARTER:HALF]))
         join_right(1, 0, 2)
+        quantize(0, QUARTER)
         nc.sync.dma_start(out_view[:, 0:2, HALF:], joined[:, 0:2, HALF:])
-        nc.scalar.copy(interleaved(rounded[1][:, :QUARTER, :]), by_fours(joined[:, :, columns(0)]))
-        nc.vector.tensor_tensor(interleaved(rounded[1][:, QUARTER:, :]), by_fours(truth[1][:, :, 0, :]), by_fours(truth[1][:, :, 1, :]), MULT)
+        nc.scalar.copy(interleaved(rounded[:, columns(0), :]), by_fours(joined[:, :, columns(0)]))
+        nc.vector.tensor_tensor(interleaved(rounded[:, columns(1), :]), by_fours(truth[1][:, :, 0, :]), by_fours(truth[1][:, :, 1, :]), MULT)
         join_right(1, 2, 4)
         nc.sync.dma_start(out_view[:, 2:4, HALF:], joined[:, 2:4, HALF:])
-        quantize_half(1)
+        quantize(HALF + QUARTER, V)
+        quantize(QUARTER, HALF + QUARTER)
         nc.scalar.dma_start(words_view, o_codes[:].bitcast(I32))
         out_rows = out_2[0].rearrange("(q r) c -> r q c", r=4)
         for r in range(4):

@@ -18,6 +18,7 @@ FLOPS = 2 * K * N * S
 HALF = 128
 QUARTER = 64
 SHARE = 24
+EARLY = 24
 
 
 def tile_picked_andpool_none_po_kernel(tc, x_words, x_scales, w1, offs, out_0, out_1, out_2):
@@ -58,9 +59,10 @@ def tile_picked_andpool_none_po_kernel(tc, x_words, x_scales, w1, offs, out_0, o
             dst = grouped[:, t0:t1, lo:hi, :].rearrange("p t m j -> p m j t")
             return dst, src
 
-        warm_out = keep.tile([P, 1], F32, name="warm_out")
-        nc.scalar.activation(warm_out[:], w_raw[0][:, 0, 0:1], SIGMOID)
-        nc.scalar.copy(*views(0, 64, 0, 4))
+        for pair in range(2):
+            dst, src = views(0, EARLY, 0, 4)
+            nc.scalar.copy(dst[:, :, 2 * pair : 2 * pair + 2, :], src[:, :, 2 * pair : 2 * pair + 2, :])
+        nc.scalar.copy(*views(EARLY, 64, 0, 4))
         nc.scalar.copy(*views(64, 64 + SHARE, 0, 2))
         nc.vector.tensor_copy(*views(64 + SHARE, 128, 0, 2))
         nc.vector.tensor_copy(*views(64, 128, 2, 4))

@@ -28,11 +28,11 @@ def tile_picked_andpool_none_po_kernel(tc, x_words, x_scales, w1, offs, out_0, o
         psum = ctx.enter_context(tc.psum_pool(name="psum", bufs=1))
 
         offsets = keep.tile([P, S // 16], U16, name="offsets")
-        nc.sync.dma_start(offsets[:], offs)
 
         w_view = w1.rearrange("(p j) n -> p j n", j=4)
         w_raw = [keep.tile([P, 4, N // 2], F32, name=f"w_raw{h}", align_bytes=64) for h in range(2)]
         nc.sync.dma_start(w_raw[0][:, 0:3, :], w_view[:, 0:3, : N // 2])
+        nc.sync.dma_start(offsets[:], offs)
 
         xs = keep.tile([P, T], U8, name="xs", align_bytes=64)
         nc.vector.memset(xs[:].bitcast(I32), 0)

@@ -15,7 +15,6 @@ MULT = mybir.AluOpType.mult
 P = 128
 K, T, S, V, N = 512, 1024, 512, 256, 512
 FLOPS = 2 * K * N * S
-HALF = 128
 QUARTER = 64
 SHARE = 24
 EARLY = 24
@@ -45,13 +44,13 @@ def tile_picked_andpool_none_po_kernel(tc, x_words, x_scales, w1, offs, out_0, o
         xw = keep.tile([P, T], U32, name="xw", align_bytes=64)
         nc.sync.dma_start(xw[:].bitcast(I32), x_words[0].rearrange("p n t -> p (n t)").bitcast(I32))
 
-        gs = keep.tile([P, S], U8, name="gs", align_bytes=64)
-        nc.vector.tensor_copy(gs[:], xs[:].indirect(offsets[:]))
+        gs = keep.tile([P, 4, 2, QUARTER], U8, name="gs", align_bytes=64)
+        gw = keep.tile([P, 4, 2, QUARTER], U32, name="gw", align_bytes=64)
+        nc.vector.tensor_copy(gs[:].rearrange("p q d c -> p d q c"), xs[:].indirect(offsets[:]))
 
         w_codes = keep.tile([P, 4, P], U32, name="w_codes", align_bytes=64)
         w_scales = keep.tile([P, 4, P], U8, name="w_scales", align_bytes=64)
         grouped = keep.tile([P, 4, P, 4], BF16, name="grouped", align_bytes=64)
-        paired_scales = keep.tile([P, 2, 2, QUARTER], U8, name="paired_scales", align_bytes=64)
 
         def views(lo, hi, t0, t1):
             h = lo // 64
@@ -66,11 +65,6 @@ def tile_picked_andpool_none_po_kernel(tc, x_words, x_scales, w1, offs, out_0, o
         nc.scalar.copy(*views(64, 64 + SHARE, 0, 2))
         nc.vector.tensor_copy(*views(64 + SHARE, 128, 0, 2))
         nc.vector.tensor_copy(*views(64, 128, 2, 4))
-        for q in range(2):
-            nc.sync.dma_start(
-                paired_scales[:, q].bitcast(I32),
-                gs[:].bitcast(I32).rearrange("p (d q c) -> p q d c", d=2, q=4)[:, 2 + q],
-            )
         for u in range(2):
             nc.vector.quantize_mx(
                 out=w_codes[:, 2 * u : 2 * u + 2, :].rearrange("p t m -> p (t m)").bitcast(FP8X4),
@@ -78,98 +72,82 @@ def tile_picked_andpool_none_po_kernel(tc, x_words, x_scales, w1, offs, out_0, o
                 in_=grouped[:, 2 * u : 2 * u + 2].rearrange("p t m j -> p (t m j)"),
             )
 
-        def pick(dst, h, d):
-            first = V * d + HALF * h
-            nc.vector.tensor_copy(dst, xw[:].indirect(offsets[:, first // 16 : (first + HALF) // 16]))
-
-        plain = [keep.tile([P, HALF], U32, name=f"plain{d}", align_bytes=64) for d in range(2)]
-        paired = keep.tile([P, 2, 2, QUARTER], U32, name="paired", align_bytes=64)
-        for d in range(2):
-            pick(plain[d][:], 0, d)
-        for d in range(2):
-            pick(paired[:, :, d, :], 1, d)
+        for q0, q1 in ((0, 1), (1, 2), (2, 4)):
+            for d in range(2):
+                first, last = d * V + q0 * QUARTER, d * V + q1 * QUARTER
+                nc.vector.tensor_copy(gw[:, q0:q1, d, :], xw[:].indirect(offsets[:, first // 16 : last // 16]))
 
         o_codes = keep.tile([P, V], U32, name="o_codes", align_bytes=64)
         o_scales = keep.tile([P, V], U8, name="o_scales", align_bytes=64)
         out_view = out_0.rearrange("(p t) v -> p t v", t=4)
         words_view = out_1[0].rearrange("p n t -> p (n t)").bitcast(I32)
-        left = keep.tile([P, 4, 2, HALF], F32, name="left", align_bytes=64)
-        truth = [keep.tile([P, 4, 2, QUARTER], F32, name=f"truth{q}", align_bytes=64) for q in range(2)]
+        truth = [keep.tile([P, 4, 2, QUARTER], F32, name=f"truth{q}", align_bytes=64) for q in range(4)]
         joined = keep.tile([P, 4, V], F32, name="joined", align_bytes=64)
         rounded = keep.tile([P, V, 4], BF16, name="rounded", align_bytes=64)
 
-        def product(dst, t, codes, scales):
-            nc.tensor.matmul_mx(
-                out=dst,
-                lhsT=w_codes[:, t, :].bitcast(FP8X4),
-                lhsT_scale=w_scales[:, t, :],
-                rhs=codes.bitcast(FP8X4),
-                rhs_scale=scales,
-                start=True,
-                stop=True,
-            )
-
-        def left_sigmoids(name, pairs, dst):
-            bank = psum.tile([P, 2, HALF], F32, name=name)
-            for e, (t, d) in enumerate(pairs):
-                product(bank[:, e, :], t, plain[d][:], gs[:, V * d : V * d + HALF])
-            nc.scalar.activation(dst, bank[:], SIGMOID)
-
-        def right_sigmoids(name, q, lo, hi):
-            bank = psum.tile([P, 2, HALF], F32, name=name)
-            for t in range(lo, hi):
-                product(bank[:, t - lo, :], t, paired[:, q].rearrange("p d c -> p (d c)"), paired_scales[:, q].rearrange("p d c -> p (d c)"))
-            nc.scalar.activation(truth[q][:, lo:hi].rearrange("p t d c -> p t (d c)"), bank[:, : hi - lo, :], SIGMOID)
-
-        def join_left(lo, hi):
-            nc.vector.tensor_tensor(joined[:, lo:hi, :HALF], left[:, lo:hi, 0, :], left[:, lo:hi, 1, :], MULT)
+        def sigmoids(name, q, t0, t1):
+            bank = psum.tile([P, 2, 2 * QUARTER], F32, name=name)
+            for t in range(t0, t1):
+                nc.tensor.matmul_mx(
+                    out=bank[:, t - t0, :],
+                    lhsT=w_codes[:, t, :].bitcast(FP8X4),
+                    lhsT_scale=w_scales[:, t, :],
+                    rhs=gw[:, q].rearrange("p d c -> p (d c)").bitcast(FP8X4),
+                    rhs_scale=gs[:, q].rearrange("p d c -> p (d c)"),
+                    start=True,
+                    stop=True,
+                )
+            nc.scalar.activation(truth[q][:, t0:t1].rearrange("p t d c -> p t (d c)"), bank[:, : t1 - t0, :], SIGMOID)
 
         def columns(q):
-            return slice(HALF + QUARTER * q, HALF + QUARTER * (q + 1))
+            return slice(QUARTER * q, QUARTER * (q + 1))
 
-        def join_right(q, lo, hi):
-            nc.vector.tensor_tensor(joined[:, lo:hi, columns(q)], truth[q][:, lo:hi, 0, :], truth[q][:, lo:hi, 1, :], MULT)
+        def join(q, t0, t1):
+            nc.vector.tensor_tensor(joined[:, t0:t1, columns(q)], truth[q][:, t0:t1, 0, :], truth[q][:, t0:t1, 1, :], MULT)
 
-        def interleaved(tile):
-            return tile.rearrange("p (c i) t -> p c t i", i=4)
+        def interleaved(q):
+            return rounded[:, columns(q), :].rearrange("p (c i) t -> p c t i", i=4)
 
         def by_fours(rows):
             return rows.rearrange("p t (c i) -> p c t i", i=4)
 
-        def quantize(lo, hi):
+        def quantize(q0, q1):
+            lo, hi = QUARTER * q0, QUARTER * q1
             nc.vector.quantize_mx(
                 out=o_codes[:, lo:hi].bitcast(FP8X4),
                 scales=o_scales[:, lo:hi],
                 in_=rounded[:, lo:hi, :].rearrange("p v t -> p (v t)"),
             )
 
-        left_sigmoids("bank0", [(0, 0), (1, 0)], left[:, 0:2, 0, :])
-        left_sigmoids("bank1", [(0, 1), (1, 1)], left[:, 0:2, 1, :])
-        left_sigmoids("bank2", [(2, 0), (2, 1)], left[:, 2, :, :])
-        left_sigmoids("bank3", [(3, 0), (3, 1)], left[:, 3, :, :])
-        right_sigmoids("bank4", 0, 0, 2)
-        right_sigmoids("bank5", 0, 2, 4)
-        right_sigmoids("bank6", 1, 0, 2)
-        right_sigmoids("bank0", 1, 2, 3)
-        right_sigmoids("bank7", 1, 3, 4)
+        sigmoids("bank0", 0, 0, 1)
+        sigmoids("bank7", 0, 1, 2)
+        sigmoids("bank1", 0, 2, 4)
+        for q in range(1, 3):
+            sigmoids(f"bank{2 * q}", q, 0, 2)
+            sigmoids(f"bank{2 * q + 1}", q, 2, 4)
+        sigmoids("bank6", 3, 0, 2)
+        sigmoids("bank0", 3, 2, 3)
+        sigmoids("bank7", 3, 3, 4)
 
-        join_left(0, 2)
-        join_left(2, 3)
-        join_left(3, 4)
-        nc.sync.dma_start(out_view[:, :, :HALF], joined[:, :, :HALF])
-        join_right(0, 0, 2)
-        nc.vector.tensor_copy(interleaved(rounded[:, :QUARTER, :]), by_fours(joined[:, :, :QUARTER]))
-        join_right(0, 2, 4)
-        nc.vector.tensor_copy(interleaved(rounded[:, QUARTER:HALF, :]), by_fours(joined[:, :, QUARTER:HALF]))
-        join_right(1, 0, 2)
-        quantize(0, QUARTER)
-        nc.sync.dma_start(out_view[:, 0:2, HALF:], joined[:, 0:2, HALF:])
-        nc.scalar.copy(interleaved(rounded[:, columns(0), :]), by_fours(joined[:, :, columns(0)]))
-        nc.vector.tensor_tensor(interleaved(rounded[:, columns(1), :]), by_fours(truth[1][:, :, 0, :]), by_fours(truth[1][:, :, 1, :]), MULT)
-        join_right(1, 2, 4)
-        nc.sync.dma_start(out_view[:, 2:4, HALF:], joined[:, 2:4, HALF:])
-        quantize(HALF + QUARTER, V)
-        quantize(QUARTER, HALF + QUARTER)
+        join(0, 0, 2)
+        join(0, 2, 4)
+        join(1, 0, 2)
+        nc.vector.tensor_copy(interleaved(0), by_fours(joined[:, :, columns(0)]))
+        join(1, 2, 4)
+        nc.sync.dma_start(out_view[:, :, :128], joined[:, :, :128])
+        join(2, 0, 2)
+        quantize(0, 1)
+        nc.vector.tensor_copy(interleaved(1), by_fours(joined[:, :, columns(1)]))
+        join(2, 2, 4)
+        join(3, 0, 2)
+        quantize(1, 2)
+        nc.sync.dma_start(out_view[:, 0:2, 128:], joined[:, 0:2, 128:])
+        nc.scalar.copy(interleaved(2), by_fours(joined[:, :, columns(2)]))
+        nc.vector.tensor_tensor(interleaved(3), by_fours(truth[3][:, :, 0, :]), by_fours(truth[3][:, :, 1, :]), MULT)
+        join(3, 2, 4)
+        nc.sync.dma_start(out_view[:, 2:4, 128:], joined[:, 2:4, 128:])
+        quantize(3, 4)
+        quantize(2, 3)
         nc.scalar.dma_start(words_view, o_codes[:].bitcast(I32))
         out_rows = out_2[0].rearrange("(q r) c -> r q c", r=4)
         for r in range(4):

from contextlib import ExitStack

import concourse.mybir as mybir

F32 = mybir.dt.float32
BF16 = mybir.dt.bfloat16
I32 = mybir.dt.int32
U32 = mybir.dt.uint32
U16 = mybir.dt.uint16
U8 = mybir.dt.uint8
FP8X4 = mybir.dt.float8_e4m3fn_x4
SIGMOID = mybir.ActivationFunctionType.Sigmoid
MULT = mybir.AluOpType.mult

P = 128
K, T, S, V, N = 512, 1024, 512, 256, 512
FLOPS = 2 * K * N * S
QUARTER = 64
SHARE = 24
EARLY = 24


def tile_picked_andpool_none_po_kernel(tc, x_words, x_scales, w1, offs, out_0, out_1, out_2):
    nc = tc.nc
    with ExitStack() as ctx:
        keep = ctx.enter_context(tc.tile_pool(name="keep", bufs=1))
        psum = ctx.enter_context(tc.psum_pool(name="psum", bufs=1))

        offsets = keep.tile([P, S // 16], U16, name="offsets")

        w_view = w1.rearrange("(p j) n -> p j n", j=4)
        w_raw = [keep.tile([P, 4, N // 2], F32, name=f"w_raw{h}", align_bytes=64) for h in range(2)]
        nc.sync.dma_start(w_raw[0][:, 0:3, :], w_view[:, 0:3, : N // 2])
        nc.sync.dma_start(offsets[:], offs)

        xs = keep.tile([P, T], U8, name="xs", align_bytes=64)
        nc.vector.memset(xs[:].bitcast(I32), 0)

        scale_rows = x_scales[0].rearrange("(q r) c -> r q c", r=4)
        for r in range(4):
            nc.sync.dma_start(xs[r:P:32, :].bitcast(I32), scale_rows[r].bitcast(I32))
        nc.sync.dma_start(w_raw[0][:, 3, :], w_view[:, 3, : N // 2])
        nc.sync.dma_start(w_raw[1][:], w_view[:, :, N // 2 :])
        xw = keep.tile([P, T], U32, name="xw", align_bytes=64)
        nc.sync.dma_start(xw[:].bitcast(I32), x_words[0].rearrange("p n t -> p (n t)").bitcast(I32))

        gs = keep.tile([P, 4, 2, QUARTER], U8, name="gs", align_bytes=64)
        gw = keep.tile([P, 4, 2, QUARTER], U32, name="gw", align_bytes=64)
        nc.vector.tensor_copy(gs[:].rearrange("p q d c -> p d q c"), xs[:].indirect(offsets[:]))

        w_codes = keep.tile([P, 4, P], U32, name="w_codes", align_bytes=64)
        w_scales = keep.tile([P, 4, P], U8, name="w_scales", align_bytes=64)
        grouped = keep.tile([P, 4, P, 4], BF16, name="grouped", align_bytes=64)

        def views(lo, hi, t0, t1):
            h = lo // 64
            src = w_raw[h][:].rearrange("p j (m t) -> p m j t", t=4)[:, lo - 64 * h : hi - 64 * h, :, t0:t1]
            dst = grouped[:, t0:t1, lo:hi, :].rearrange("p t m j -> p m j t")
            return dst, src

        for pair in range(2):
            dst, src = views(0, EARLY, 0, 4)
            nc.scalar.copy(dst[:, :, 2 * pair : 2 * pair + 2, :], src[:, :, 2 * pair : 2 * pair + 2, :])
        nc.scalar.copy(*views(EARLY, 64, 0, 4))
        nc.scalar.copy(*views(64, 64 + SHARE, 0, 2))
        nc.vector.tensor_copy(*views(64 + SHARE, 128, 0, 2))
        nc.vector.tensor_copy(*views(64, 128, 2, 4))
        for u in range(2):
            nc.vector.quantize_mx(
                out=w_codes[:, 2 * u : 2 * u + 2, :].rearrange("p t m -> p (t m)").bitcast(FP8X4),
                scales=w_scales[:, 2 * u : 2 * u + 2, :].rearrange("p t m -> p (t m)"),
                in_=grouped[:, 2 * u : 2 * u + 2].rearrange("p t m j -> p (t m j)"),
            )

        for q0, q1 in ((0, 1), (1, 2), (2, 4)):
            for d in range(2):
                first, last = d * V + q0 * QUARTER, d * V + q1 * QUARTER
                nc.vector.tensor_copy(gw[:, q0:q1, d, :], xw[:].indirect(offsets[:, first // 16 : last // 16]))

        o_codes = keep.tile([P, V], U32, name="o_codes", align_bytes=64)
        o_scales = keep.tile([P, V], U8, name="o_scales", align_bytes=64)
        out_view = out_0.rearrange("(p t) v -> p t v", t=4)
        words_view = out_1[0].rearrange("p n t -> p (n t)").bitcast(I32)
        truth = [keep.tile([P, 4, 2, QUARTER], F32, name=f"truth{q}", align_bytes=64) for q in range(4)]
        joined = keep.tile([P, 4, V], F32, name="joined", align_bytes=64)
        rounded = keep.tile([P, V, 4], BF16, name="rounded", align_bytes=64)

        def sigmoids(name, q, t0, t1):
            bank = psum.tile([P, 2, 2 * QUARTER], F32, name=name)
            for t in range(t0, t1):
                nc.tensor.matmul_mx(
                    out=bank[:, t - t0, :],
                    lhsT=w_codes[:, t, :].bitcast(FP8X4),
                    lhsT_scale=w_scales[:, t, :],
                    rhs=gw[:, q].rearrange("p d c -> p (d c)").bitcast(FP8X4),
                    rhs_scale=gs[:, q].rearrange("p d c -> p (d c)"),
                    start=True,
                    stop=True,
                )
            nc.scalar.activation(truth[q][:, t0:t1].rearrange("p t d c -> p t (d c)"), bank[:, : t1 - t0, :], SIGMOID)

        def columns(q):
            return slice(QUARTER * q, QUARTER * (q + 1))

        def join(q, t0, t1):
            nc.vector.tensor_tensor(joined[:, t0:t1, columns(q)], truth[q][:, t0:t1, 0, :], truth[q][:, t0:t1, 1, :], MULT)

        def interleaved(q):
            return rounded[:, columns(q), :].rearrange("p (c i) t -> p c t i", i=4)

        def by_fours(rows):
            return rows.rearrange("p t (c i) -> p c t i", i=4)

        def quantize(q0, q1):
            lo, hi = QUARTER * q0, QUARTER * q1
            nc.vector.quantize_mx(
                out=o_codes[:, lo:hi].bitcast(FP8X4),
                scales=o_scales[:, lo:hi],
                in_=rounded[:, lo:hi, :].rearrange("p v t -> p (v t)"),
            )

        sigmoids("bank0", 0, 0, 1)
        sigmoids("bank7", 0, 1, 2)
        sigmoids("bank1", 0, 2, 4)
        for q in range(1, 3):
            sigmoids(f"bank{2 * q}", q, 0, 2)
            sigmoids(f"bank{2 * q + 1}", q, 2, 4)
        sigmoids("bank6", 3, 0, 2)
        sigmoids("bank0", 3, 2, 3)
        sigmoids("bank7", 3, 3, 4)

        join(0, 0, 2)
        join(0, 2, 4)
        join(1, 0, 2)
        nc.vector.tensor_copy(interleaved(0), by_fours(joined[:, :, columns(0)]))
        join(1, 2, 4)
        nc.sync.dma_start(out_view[:, :, :128], joined[:, :, :128])
        join(2, 0, 2)
        quantize(0, 1)
        nc.vector.tensor_copy(interleaved(1), by_fours(joined[:, :, columns(1)]))
        join(2, 2, 4)
        join(3, 0, 2)
        quantize(1, 2)
        nc.sync.dma_start(out_view[:, 0:2, 128:], joined[:, 0:2, 128:])
        nc.scalar.copy(interleaved(2), by_fours(joined[:, :, columns(2)]))
        nc.vector.tensor_tensor(interleaved(3), by_fours(truth[3][:, :, 0, :]), by_fours(truth[3][:, :, 1, :]), MULT)
        join(3, 2, 4)
        nc.sync.dma_start(out_view[:, 2:4, 128:], joined[:, 2:4, 128:])
        quantize(3, 4)
        quantize(2, 3)
        nc.scalar.dma_start(words_view, o_codes[:].bitcast(I32))
        out_rows = out_2[0].rearrange("(q r) c -> r q c", r=4)
        for r in range(4):
            queue = nc.sync if r % 2 == 0 else nc.scalar
            queue.dma_start(out_rows[r].bitcast(I32), o_scales[r:P:32, :].bitcast(I32))
